import numpy as np
import ml_dtypes


def mxq(x, axis, fmt="e4m3"):
    dtype, down = {"e4m3": (ml_dtypes.float8_e4m3fn, 7), "e5m2": (ml_dtypes.float8_e5m2, 14)}[fmt]
    v = np.moveaxis(np.asarray(x, np.float32).astype(ml_dtypes.bfloat16).astype(np.float64), axis, -1)
    blocks = v.reshape(v.shape[:-1] + (-1, 32))
    amax = np.abs(blocks).max(-1, keepdims=True)
    byte = np.maximum(np.where(amax > 0, np.frexp(amax)[1] - 1 + 127, 0) - down, 1)
    scale = np.exp2(byte - 127.0)
    codes = (blocks / scale).astype(np.float32).astype(dtype).astype(np.float64)
    return np.moveaxis((codes * scale).reshape(v.shape), -1, axis)


WIDE = False


def mx_kscale(k):
    if not WIDE:
        return np.ones(k)
    levels = np.array([30, -30])
    if k % 512:
        return np.exp2(np.random.permutation(np.resize(levels, k // 32))).repeat(32)
    a = np.empty((k // 512, 16))
    for p in range(k // 512):
        a[p, :8] = np.random.permutation(np.resize(levels, 8))
        for g in range(8):
            far = levels[np.abs(levels - a[p, g]) >= 10]
            a[p, g + 8] = far[np.random.randint(len(far))]
    return np.exp2(a.ravel()).repeat(32)


def f64(x):
    return np.asarray(x).astype(np.float64)


def planes(y):
    n, m = y.shape
    v = y.astype(np.float32).astype(ml_dtypes.bfloat16).astype(np.float64).reshape(n // 32, 32, m)
    top = np.abs(v).max(1)
    byte = np.clip(np.where(top > 0, np.frexp(top)[1] - 1 + 127 - 7, 1), 1, 254)
    codes = (v * np.exp2(127.0 - byte)[:, None, :]).reshape(n, m).astype(np.float32).astype(ml_dtypes.float8_e4m3fn).view(np.uint8)
    words = codes.reshape(n // 512, 128, 4, m).transpose(0, 1, 3, 2)
    return np.ascontiguousarray(words), np.ascontiguousarray(byte.astype(np.uint8).reshape(n // 512, 16, m))


K, L, M, T = 512, 512, 1536, 1024


def setup_inputs():
    n = np.random.standard_normal
    s1 = mx_kscale(K)[:, None]
    s2 = mx_kscale(L)[:, None]
    m = np.exp(0.5 * n((1, T)))
    return {
        "w": (n((K, M)) / np.sqrt(K) / s1).astype(np.float32),
        "dy": (m * n((K, T)) * s1).astype(np.float32),
        "v": (n((L, M)) / np.sqrt(L) / s2).astype(np.float32),
        "e": (n((L, T)) * s2).astype(np.float32),
        "g": (n((1536, 1024))).astype(np.float32),
    }


def reference(w, dy, v, e, g):
    w_ = mxq(f64(w), 0, "e4m3")
    dy_ = mxq(f64(dy), 0, "e5m2")
    v_ = mxq(f64(v), 0, "e4m3")
    e_ = mxq(f64(e), 0, "e4m3")
    y = w_.T @ dy_ + v_.T @ e_
    out_0 = f64(g) * y
    return (out_0,) + planes(out_0)

@@ -1,0 +1,195 @@
+from contextlib import ExitStack
+
+import concourse.mybir as mybir
+
+K, M, T = 512, 1536, 1024
+FLOPS = 2 * 2 * K * M * T
+
+F32 = mybir.dt.float32
+BF16 = mybir.dt.bfloat16
+U32 = mybir.dt.uint32
+I32 = mybir.dt.int32
+U8 = mybir.dt.uint8
+E4M3 = mybir.dt.float8_e4m3fn_x4
+E5M2 = mybir.dt.float8_e5m2_x4
+
+P = 128
+PACK = 4
+W = 512
+BLOCKS = M // W
+HALVES = T // W
+
+
+def tile_mix_aux_fm_pl_mul_kernel(tc, w, dy, v, e, g, out_0, out_1, out_2):
+    nc = tc.nc
+    with ExitStack() as ctx:
+        keep = ctx.enter_context(tc.tile_pool(name="keep", bufs=1))
+        stage = ctx.enter_context(tc.tile_pool(name="stage", bufs=4))
+        psum = ctx.enter_context(tc.psum_pool(name="psum", bufs=1))
+        ctx.enter_context(tc.manual_schedule())
+
+        def load(name, rows):
+            raw = keep.tile([P, PACK, rows.shape[1]], F32, name=name)
+            nc.sync.dma_start(out=raw[:], in_=rows.rearrange("(p j) c -> p j c", j=PACK))
+            return raw
+
+        dy_raw = load("dy_raw", dy)
+        w_raw = load("w_raw", w)
+        e_raw = load("e_raw", e)
+        v_first = load("v_first", v[:, 0:W])
+        g0 = load("g0", g[0:W, :])
+        v_rest = load("v_rest", v[:, W:M])
+        g1 = load("g1", g[W : 2 * W, :])
+        g2 = load("g2", g[2 * W : 3 * W, :])
+        result = [g0, g1, g2]
+
+        dy_codes = keep.tile([P, T], U32, align_bytes=64)
+        dy_scales = keep.tile([P, T], U8, align_bytes=64)
+        e_codes = keep.tile([P, T], U32, align_bytes=64)
+        e_scales = keep.tile([P, T], U8, align_bytes=64)
+        w_codes = keep.tile([P, M], U32, align_bytes=64)
+        w_scales = keep.tile([P, M], U8, align_bytes=64)
+        v_codes = keep.tile([P, M], U32, align_bytes=64)
+        v_scales = keep.tile([P, M], U8, align_bytes=64)
+        out_codes = keep.tile([P, BLOCKS, T], U32, align_bytes=64)
+        out_scales = keep.tile([P, BLOCKS, T], U8, align_bytes=64)
+
+        def cols(n):
+            return slice(n * W, (n + 1) * W)
+
+        def interleave(copy, tag, raw):
+            grouped = stage.tile([P, W * PACK], BF16, name=tag, align_bytes=64)
+            copy(
+                out=grouped[:].rearrange("p (c i j) -> p c j i", i=4, j=PACK),
+                in_=raw.rearrange("p j (c i) -> p c j i", i=4),
+            )
+            return grouped
+
+        def deal(copy, raw):
+            grouped = stage.tile([P, W * PACK], BF16, name="operand", align_bytes=64)
+            copy(
+                out=grouped[:].rearrange("p (r m j) -> p m r j", r=PACK, j=PACK),
+                in_=raw.rearrange("p j (m r) -> p m r j", r=PACK),
+            )
+            return grouped
+
+        def quantize(grouped, codes, scales, fmt):
+            nc.vector.quantize_mx(out=codes.bitcast(fmt), scales=scales, in_=grouped[:])
+
+        on_vector, on_scalar = nc.vector.tensor_copy, nc.scalar.copy
+
+        banks = {}
+
+        def main_pass(a, h, r):
+            acc = psum.tile([P, W], F32, name="bank%d" % (h * PACK + r))
+            banks[(a, h, r)] = acc
+            m_cols = slice(a * W + r * P, a * W + (r + 1) * P)
+            nc.tensor.matmul_mx(
+                out=acc[:],
+                lhsT=w_codes[:, m_cols].bitcast(E4M3),
+                lhsT_scale=w_scales[:, m_cols],
+                rhs=dy_codes[:, cols(h)].bitcast(E5M2),
+                rhs_scale=dy_scales[:, cols(h)],
+                start=True,
+                stop=False,
+            )
+
+        def aux_pass(a, h, r):
+            m_cols = slice(a * W + r * P, a * W + (r + 1) * P)
+            nc.tensor.matmul_mx(
+                out=banks[(a, h, r)][:],
+                lhsT=v_codes[:, m_cols].bitcast(E4M3),
+                lhsT_scale=v_scales[:, m_cols],
+                rhs=e_codes[:, cols(h)].bitcast(E4M3),
+                rhs_scale=e_scales[:, cols(h)],
+                start=False,
+                stop=True,
+            )
+
+        order = [(h, r) for h in range(HALVES) for r in range(PACK)]
+
+        def gate(a, h):
+            for r in range(PACK):
+                nc.vector.tensor_tensor(
+                    out=result[a][:, r, cols(h)],
+                    in0=banks[(a, h, r)][:],
+                    in1=result[a][:, r, cols(h)],
+                    op=mybir.AluOpType.mult,
+                )
+
+        def round_result(a):
+            return [interleave(on_scalar, "rounded", result[a][:, :, cols(h)]) for h in range(HALVES)]
+
+        def quantize_result(a, h, grouped):
+            quantize(grouped, out_codes[:, a, cols(h)], out_scales[:, a, cols(h)], E4M3)
+
+        def store_result(a):
+            nc.sync.dma_start(out=out_0[cols(a), :].rearrange("(p j) c -> p j c", j=PACK), in_=result[a][:])
+
+        def store_codes(a):
+            nc.sync.dma_start(
+                out=out_1[a].rearrange("p t j -> p (t j)").bitcast(I32), in_=out_codes[:, a, :].bitcast(I32)
+            )
+
+        dy0 = interleave(on_vector, "operand", dy_raw[:, :, cols(0)])
+        dy1 = interleave(on_scalar, "operand", dy_raw[:, :, cols(1)])
+        quantize(dy0, dy_codes[:, cols(0)], dy_scales[:, cols(0)], E5M2)
+        quantize(dy1, dy_codes[:, cols(1)], dy_scales[:, cols(1)], E5M2)
+        w0 = deal(on_vector, w_raw[:, :, cols(0)])
+        w1 = deal(on_scalar, w_raw[:, :, cols(1)])
+        w2 = deal(on_vector, w_raw[:, :, cols(2)])
+        quantize(w0, w_codes[:, cols(0)], w_scales[:, cols(0)], E4M3)
+        quantize(w2, w_codes[:, cols(2)], w_scales[:, cols(2)], E4M3)
+        quantize(w1, w_codes[:, cols(1)], w_scales[:, cols(1)], E4M3)
+        for h, r in order:
+            main_pass(0, h, r)
+        e0 = interleave(on_vector, "operand", e_raw[:, :, cols(0)])
+        e1 = interleave(on_scalar, "operand", e_raw[:, :, cols(1)])
+        quantize(e0, e_codes[:, cols(0)], e_scales[:, cols(0)], E4M3)
+        v0 = deal(on_vector, v_first[:])
+        quantize(e1, e_codes[:, cols(1)], e_scales[:, cols(1)], E4M3)
+        quantize(v0, v_codes[:, cols(0)], v_scales[:, cols(0)], E4M3)
+
+        for h, r in order:
+            aux_pass(0, h, r)
+        gate(0, 0)
+        gate(0, 1)
+        store_result(0)
+        rounded0 = round_result(0)
+        for h, r in order:
+            main_pass(1, h, r)
+        v1 = deal(on_vector, v_rest[:, :, cols(0)])
+        v2 = deal(on_scalar, v_rest[:, :, cols(1)])
+        quantize_result(0, 0, rounded0[0])
+        quantize(v1, v_codes[:, cols(1)], v_scales[:, cols(1)], E4M3)
+        quantize_result(0, 1, rounded0[1])
+        store_codes(0)
+
+        for h, r in order:
+            aux_pass(1, h, r)
+        gate(1, 0)
+        quantize(v2, v_codes[:, cols(2)], v_scales[:, cols(2)], E4M3)
+        gate(1, 1)
+        store_result(1)
+        rounded1 = round_result(1)
+
+        for h, r in order:
+            main_pass(2, h, r)
+            aux_pass(2, h, r)
+        gate(2, 0)
+        quantize_result(1, 0, rounded1[0])
+        gate(2, 1)
+        quantize_result(1, 1, rounded1[1])
+        store_codes(1)
+        store_result(2)
+        rounded2 = round_result(2)
+        quantize_result(2, 0, rounded2[0])
+        quantize_result(2, 1, rounded2[1])
+
+        scale_rows = out_2.bitcast(I32)
+        for q in range(4):
+            nc.sync.dma_start(
+                out=scale_rows[:, 4 * q : 4 * q + 4, :].rearrange("a r n -> r a n"),
+                in_=out_scales[32 * q : 32 * q + 4, :, :].bitcast(I32),
+            )
+        store_codes(2)

@@ -52,7 +52,7 @@ def tile_mix_aux_fm_pl_mul_kernel(tc, w, dy, v, e, g, out_0, out_1, out_2):
         v_codes = keep.tile([P, M], U32, align_bytes=64)
         v_scales = keep.tile([P, M], U8, align_bytes=64)
         out_codes = keep.tile([P, BLOCKS, T], U32, align_bytes=64)
-        out_scales = keep.tile([P, BLOCKS, T], U8, align_bytes=64)
+        out_scales = keep.tile([P, T], U8, align_bytes=64)
 
         def cols(n):
             return slice(n * W, (n + 1) * W)
@@ -121,14 +121,15 @@ def tile_mix_aux_fm_pl_mul_kernel(tc, w, dy, v, e, g, out_0, out_1, out_2):
             return [interleave(on_scalar, "rounded", result[a][:, :, cols(h)]) for h in range(HALVES)]
 
         def quantize_result(a, h, grouped):
-            quantize(grouped, out_codes[:, a, cols(h)], out_scales[:, a, cols(h)], E4M3)
+            quantize(grouped, out_codes[:, a, cols(h)], out_scales[4 * a : P, cols(h)], E4M3)
 
         def store_result(a):
             nc.sync.dma_start(out=out_0[cols(a), :].rearrange("(p j) c -> p j c", j=PACK), in_=result[a][:])
 
-        def store_codes(a):
+        def store_codes(first, last):
             nc.sync.dma_start(
-                out=out_1[a].rearrange("p t j -> p (t j)").bitcast(I32), in_=out_codes[:, a, :].bitcast(I32)
+                out=out_1[first:last].rearrange("a p t j -> p a (t j)").bitcast(I32),
+                in_=out_codes[:, first:last, :].bitcast(I32),
             )
 
         dy0 = interleave(on_vector, "operand", dy_raw[:, :, cols(0)])
@@ -159,16 +160,16 @@ def tile_mix_aux_fm_pl_mul_kernel(tc, w, dy, v, e, g, out_0, out_1, out_2):
         for h, r in order:
             main_pass(1, h, r)
         v1 = deal(on_vector, v_rest[:, :, cols(0)])
-        v2 = deal(on_scalar, v_rest[:, :, cols(1)])
         quantize_result(0, 0, rounded0[0])
         quantize(v1, v_codes[:, cols(1)], v_scales[:, cols(1)], E4M3)
+        v2 = deal(on_vector, v_rest[:, :, cols(1)])
         quantize_result(0, 1, rounded0[1])
-        store_codes(0)
+        quantize(v2, v_codes[:, cols(2)], v_scales[:, cols(2)], E4M3)
+        store_codes(0, 1)
 
         for h, r in order:
             aux_pass(1, h, r)
         gate(1, 0)
-        quantize(v2, v_codes[:, cols(2)], v_scales[:, cols(2)], E4M3)
         gate(1, 1)
         store_result(1)
         rounded1 = round_result(1)
@@ -177,19 +178,18 @@ def tile_mix_aux_fm_pl_mul_kernel(tc, w, dy, v, e, g, out_0, out_1, out_2):
             main_pass(2, h, r)
             aux_pass(2, h, r)
         gate(2, 0)
-        quantize_result(1, 0, rounded1[0])
         gate(2, 1)
-        quantize_result(1, 1, rounded1[1])
-        store_codes(1)
         store_result(2)
         rounded2 = round_result(2)
+        quantize_result(1, 0, rounded1[0])
+        quantize_result(1, 1, rounded1[1])
         quantize_result(2, 0, rounded2[0])
         quantize_result(2, 1, rounded2[1])
+        store_codes(1, 3)
 
         scale_rows = out_2.bitcast(I32)
         for q in range(4):
-            nc.sync.dma_start(
-                out=scale_rows[:, 4 * q : 4 * q + 4, :].rearrange("a r n -> r a n"),
-                in_=out_scales[32 * q : 32 * q + 4, :, :].bitcast(I32),
+            nc.gpsimd.dma_start(
+                out=scale_rows[:, 4 * q : 4 * q + 4, :],
+                in_=out_scales[32 * q : 32 * q + 4 * BLOCKS, :].bitcast(I32),
             )
-        store_codes(2)

@@ -41,7 +41,11 @@ def tile_mix_aux_fm_pl_mul_kernel(tc, w, dy, v, e, g, out_0, out_1, out_2):
         v_rest = load("v_rest", v[:, W:M])
         g1 = load("g1", g[W : 2 * W, :])
         g2 = load("g2", g[2 * W : 3 * W, :])
-        result = [g0, g1, g2]
+        gates = [g0, g1, g2]
+        last = [keep.tile([P, PACK, W], F32, name="last%d" % h) for h in range(HALVES)]
+
+        def result(a, h):
+            return last[h][:] if a == BLOCKS - 1 else gates[a][:, :, cols(h)]
 
         dy_codes = keep.tile([P, T], U32, align_bytes=64)
         dy_scales = keep.tile([P, T], U8, align_bytes=64)
@@ -111,20 +115,25 @@ def tile_mix_aux_fm_pl_mul_kernel(tc, w, dy, v, e, g, out_0, out_1, out_2):
         def gate(a, h):
             for r in range(PACK):
                 nc.vector.tensor_tensor(
-                    out=result[a][:, r, cols(h)],
+                    out=result(a, h)[:, r, :],
                     in0=banks[(a, h, r)][:],
-                    in1=result[a][:, r, cols(h)],
+                    in1=gates[a][:, r, cols(h)],
                     op=mybir.AluOpType.mult,
                 )
 
         def round_result(a):
-            return [interleave(on_scalar, "rounded", result[a][:, :, cols(h)]) for h in range(HALVES)]
+            return [interleave(on_scalar, "rounded", result(a, h)) for h in range(HALVES)]
 
         def quantize_result(a, h, grouped):
             quantize(grouped, out_codes[:, a, cols(h)], out_scales[4 * a : P, cols(h)], E4M3)
 
         def store_result(a):
-            nc.sync.dma_start(out=out_0[cols(a), :].rearrange("(p j) c -> p j c", j=PACK), in_=result[a][:])
+            nc.sync.dma_start(out=out_0[cols(a), :].rearrange("(p j) c -> p j c", j=PACK), in_=gates[a][:])
+
+        def store_last(h):
+            nc.sync.dma_start(
+                out=out_0[cols(BLOCKS - 1), cols(h)].rearrange("(p j) c -> p j c", j=PACK), in_=last[h][:]
+            )
 
         def store_codes(first, last):
             nc.sync.dma_start(
@@ -165,7 +174,6 @@ def tile_mix_aux_fm_pl_mul_kernel(tc, w, dy, v, e, g, out_0, out_1, out_2):
         v2 = deal(on_vector, v_rest[:, :, cols(1)])
         quantize_result(0, 1, rounded0[1])
         quantize(v2, v_codes[:, cols(2)], v_scales[:, cols(2)], E4M3)
-        store_codes(0, 1)
 
         for h, r in order:
             aux_pass(1, h, r)
@@ -178,14 +186,15 @@ def tile_mix_aux_fm_pl_mul_kernel(tc, w, dy, v, e, g, out_0, out_1, out_2):
             main_pass(2, h, r)
             aux_pass(2, h, r)
         gate(2, 0)
+        store_last(0)
         gate(2, 1)
-        store_result(2)
+        store_last(1)
         rounded2 = round_result(2)
         quantize_result(1, 0, rounded1[0])
         quantize_result(1, 1, rounded1[1])
         quantize_result(2, 0, rounded2[0])
         quantize_result(2, 1, rounded2[1])
-        store_codes(1, 3)
+        store_codes(0, 3)
 
         scale_rows = out_2.bitcast(I32)
         for q in range(4):

@@ -42,10 +42,12 @@ def tile_mix_aux_fm_pl_mul_kernel(tc, w, dy, v, e, g, out_0, out_1, out_2):
         g1 = load("g1", g[W : 2 * W, :])
         g2 = load("g2", g[2 * W : 3 * W, :])
         gates = [g0, g1, g2]
-        last = [keep.tile([P, PACK, W], F32, name="last%d" % h) for h in range(HALVES)]
+        halves = {
+            (a, h): keep.tile([P, PACK, W], F32, name="half%d%d" % (a, h)) for a in (1, 2) for h in range(HALVES)
+        }
 
         def result(a, h):
-            return last[h][:] if a == BLOCKS - 1 else gates[a][:, :, cols(h)]
+            return halves[(a, h)][:] if a > 0 else gates[a][:, :, cols(h)]
 
         dy_codes = keep.tile([P, T], U32, align_bytes=64)
         dy_scales = keep.tile([P, T], U8, align_bytes=64)
@@ -130,9 +132,9 @@ def tile_mix_aux_fm_pl_mul_kernel(tc, w, dy, v, e, g, out_0, out_1, out_2):
         def store_result(a):
             nc.sync.dma_start(out=out_0[cols(a), :].rearrange("(p j) c -> p j c", j=PACK), in_=gates[a][:])
 
-        def store_last(h):
+        def store_half(a, h):
             nc.sync.dma_start(
-                out=out_0[cols(BLOCKS - 1), cols(h)].rearrange("(p j) c -> p j c", j=PACK), in_=last[h][:]
+                out=out_0[cols(a), cols(h)].rearrange("(p j) c -> p j c", j=PACK), in_=result(a, h)
             )
 
         def store_codes(first, last):
@@ -178,17 +180,18 @@ def tile_mix_aux_fm_pl_mul_kernel(tc, w, dy, v, e, g, out_0, out_1, out_2):
         for h, r in order:
             aux_pass(1, h, r)
         gate(1, 0)
+        store_half(1, 0)
         gate(1, 1)
-        store_result(1)
+        store_half(1, 1)
         rounded1 = round_result(1)
 
         for h, r in order:
             main_pass(2, h, r)
             aux_pass(2, h, r)
         gate(2, 0)
-        store_last(0)
+        store_half(2, 0)
         gate(2, 1)
-        store_last(1)
+        store_half(2, 1)
         rounded2 = round_result(2)
         quantize_result(1, 0, rounded1[0])
         quantize_result(1, 1, rounded1[1])

@@ -171,11 +171,11 @@ def tile_mix_aux_fm_pl_mul_kernel(tc, w, dy, v, e, g, out_0, out_1, out_2):
         for h, r in order:
             main_pass(1, h, r)
         v1 = deal(on_vector, v_rest[:, :, cols(0)])
-        quantize_result(0, 0, rounded0[0])
-        quantize(v1, v_codes[:, cols(1)], v_scales[:, cols(1)], E4M3)
         v2 = deal(on_vector, v_rest[:, :, cols(1)])
-        quantize_result(0, 1, rounded0[1])
+        quantize(v1, v_codes[:, cols(1)], v_scales[:, cols(1)], E4M3)
+        quantize_result(0, 0, rounded0[0])
         quantize(v2, v_codes[:, cols(2)], v_scales[:, cols(2)], E4M3)
+        quantize_result(0, 1, rounded0[1])
 
         for h, r in order:
             aux_pass(1, h, r)
@@ -201,7 +201,8 @@ def tile_mix_aux_fm_pl_mul_kernel(tc, w, dy, v, e, g, out_0, out_1, out_2):
 
         scale_rows = out_2.bitcast(I32)
         for q in range(4):
-            nc.gpsimd.dma_start(
+            queue = nc.gpsimd if q % 2 == 0 else nc.scalar
+            queue.dma_start(
                 out=scale_rows[:, 4 * q : 4 * q + 4, :],
                 in_=out_scales[32 * q : 32 * q + 4 * BLOCKS, :].bitcast(I32),
             )

@@ -36,18 +36,11 @@ def tile_mix_aux_fm_pl_mul_kernel(tc, w, dy, v, e, g, out_0, out_1, out_2):
         dy_raw = load("dy_raw", dy)
         w_raw = load("w_raw", w)
         e_raw = load("e_raw", e)
-        v_first = load("v_first", v[:, 0:W])
-        g0 = load("g0", g[0:W, :])
-        v_rest = load("v_rest", v[:, W:M])
-        g1 = load("g1", g[W : 2 * W, :])
-        g2 = load("g2", g[2 * W : 3 * W, :])
-        gates = [g0, g1, g2]
-        halves = {
-            (a, h): keep.tile([P, PACK, W], F32, name="half%d%d" % (a, h)) for a in (1, 2) for h in range(HALVES)
-        }
+        v_raw = load("v_raw", v)
+        gates = [load("g%d" % a, g[a * W : (a + 1) * W, :]) for a in range(BLOCKS)]
 
         def result(a, h):
-            return halves[(a, h)][:] if a > 0 else gates[a][:, :, cols(h)]
+            return gates[a][:, :, cols(h)]
 
         dy_codes = keep.tile([P, T], U32, align_bytes=64)
         dy_scales = keep.tile([P, T], U8, align_bytes=64)
@@ -132,11 +125,6 @@ def tile_mix_aux_fm_pl_mul_kernel(tc, w, dy, v, e, g, out_0, out_1, out_2):
         def store_result(a):
             nc.sync.dma_start(out=out_0[cols(a), :].rearrange("(p j) c -> p j c", j=PACK), in_=gates[a][:])
 
-        def store_half(a, h):
-            nc.sync.dma_start(
-                out=out_0[cols(a), cols(h)].rearrange("(p j) c -> p j c", j=PACK), in_=result(a, h)
-            )
-
         def store_codes(first, last):
             nc.sync.dma_start(
                 out=out_1[first:last].rearrange("a p t j -> p a (t j)").bitcast(I32),
@@ -158,9 +146,13 @@ def tile_mix_aux_fm_pl_mul_kernel(tc, w, dy, v, e, g, out_0, out_1, out_2):
         e0 = interleave(on_vector, "operand", e_raw[:, :, cols(0)])
         e1 = interleave(on_scalar, "operand", e_raw[:, :, cols(1)])
         quantize(e0, e_codes[:, cols(0)], e_scales[:, cols(0)], E4M3)
-        v0 = deal(on_vector, v_first[:])
         quantize(e1, e_codes[:, cols(1)], e_scales[:, cols(1)], E4M3)
+        v0 = deal(on_vector, v_raw[:, :, cols(0)])
+        v1 = deal(on_scalar, v_raw[:, :, cols(1)])
+        v2 = deal(on_vector, v_raw[:, :, cols(2)])
         quantize(v0, v_codes[:, cols(0)], v_scales[:, cols(0)], E4M3)
+        quantize(v2, v_codes[:, cols(2)], v_scales[:, cols(2)], E4M3)
+        quantize(v1, v_codes[:, cols(1)], v_scales[:, cols(1)], E4M3)
 
         for h, r in order:
             aux_pass(0, h, r)
@@ -168,35 +160,29 @@ def tile_mix_aux_fm_pl_mul_kernel(tc, w, dy, v, e, g, out_0, out_1, out_2):
         gate(0, 1)
         store_result(0)
         rounded0 = round_result(0)
-        for h, r in order:
-            main_pass(1, h, r)
-        v1 = deal(on_vector, v_rest[:, :, cols(0)])
-        v2 = deal(on_vector, v_rest[:, :, cols(1)])
-        quantize(v1, v_codes[:, cols(1)], v_scales[:, cols(1)], E4M3)
-        quantize_result(0, 0, rounded0[0])
-        quantize(v2, v_codes[:, cols(2)], v_scales[:, cols(2)], E4M3)
-        quantize_result(0, 1, rounded0[1])
 
         for h, r in order:
+            main_pass(1, h, r)
             aux_pass(1, h, r)
         gate(1, 0)
-        store_half(1, 0)
         gate(1, 1)
-        store_half(1, 1)
+        store_result(1)
         rounded1 = round_result(1)
 
         for h, r in order:
             main_pass(2, h, r)
             aux_pass(2, h, r)
         gate(2, 0)
-        store_half(2, 0)
         gate(2, 1)
-        store_half(2, 1)
-        rounded2 = round_result(2)
+        store_result(2)
+        quantize_result(0, 0, rounded0[0])
+        quantize_result(0, 1, rounded0[1])
+        last0 = interleave(on_scalar, "rounded", result(2, 0))
+        last1 = interleave(on_vector, "rounded", result(2, 1))
         quantize_result(1, 0, rounded1[0])
         quantize_result(1, 1, rounded1[1])
-        quantize_result(2, 0, rounded2[0])
-        quantize_result(2, 1, rounded2[1])
+        quantize_result(2, 1, last1)
+        quantize_result(2, 0, last0)
         store_codes(0, 3)
 
         scale_rows = out_2.bitcast(I32)

@@ -29,7 +29,7 @@ def tile_mix_aux_fm_pl_mul_kernel(tc, w, dy, v, e, g, out_0, out_1, out_2):
         ctx.enter_context(tc.manual_schedule())
 
         def load(name, rows):
-            raw = keep.tile([P, PACK, rows.shape[1]], F32, name=name)
+            raw = keep.tile([P, PACK, rows.shape[1]], F32, name=name, align_bytes=256)
             nc.sync.dma_start(out=raw[:], in_=rows.rearrange("(p j) c -> p j c", j=PACK))
             return raw
 
@@ -50,8 +50,8 @@ def tile_mix_aux_fm_pl_mul_kernel(tc, w, dy, v, e, g, out_0, out_1, out_2):
         w_scales = keep.tile([P, M], U8, align_bytes=64)
         v_codes = keep.tile([P, M], U32, align_bytes=64)
         v_scales = keep.tile([P, M], U8, align_bytes=64)
-        out_codes = keep.tile([P, BLOCKS, T], U32, align_bytes=64)
-        out_scales = keep.tile([P, T], U8, align_bytes=64)
+        out_codes = keep.tile([P, BLOCKS, T], U32, align_bytes=256)
+        out_scales = keep.tile([P, T], U8, align_bytes=256)
 
         def cols(n):
             return slice(n * W, (n + 1) * W)

@@ -187,8 +187,7 @@ def tile_mix_aux_fm_pl_mul_kernel(tc, w, dy, v, e, g, out_0, out_1, out_2):
 
         scale_rows = out_2.bitcast(I32)
         for q in range(4):
-            queue = nc.gpsimd if q % 2 == 0 else nc.scalar
-            queue.dma_start(
+            nc.scalar.dma_start(
                 out=scale_rows[:, 4 * q : 4 * q + 4, :],
                 in_=out_scales[32 * q : 32 * q + 4 * BLOCKS, :].bitcast(I32),
             )

@@ -187,7 +187,7 @@ def tile_mix_aux_fm_pl_mul_kernel(tc, w, dy, v, e, g, out_0, out_1, out_2):
 
         scale_rows = out_2.bitcast(I32)
         for q in range(4):
-            nc.scalar.dma_start(
+            nc.sync.dma_start(
                 out=scale_rows[:, 4 * q : 4 * q + 4, :],
                 in_=out_scales[32 * q : 32 * q + 4 * BLOCKS, :].bitcast(I32),
             )

@@ -29,7 +29,7 @@ def tile_mix_aux_fm_pl_mul_kernel(tc, w, dy, v, e, g, out_0, out_1, out_2):
         ctx.enter_context(tc.manual_schedule())
 
         def load(name, rows):
-            raw = keep.tile([P, PACK, rows.shape[1]], F32, name=name, align_bytes=256)
+            raw = keep.tile([P, PACK, rows.shape[1]], F32, name=name, align_bytes=4096)
             nc.sync.dma_start(out=raw[:], in_=rows.rearrange("(p j) c -> p j c", j=PACK))
             return raw
 
@@ -50,8 +50,8 @@ def tile_mix_aux_fm_pl_mul_kernel(tc, w, dy, v, e, g, out_0, out_1, out_2):
         w_scales = keep.tile([P, M], U8, align_bytes=64)
         v_codes = keep.tile([P, M], U32, align_bytes=64)
         v_scales = keep.tile([P, M], U8, align_bytes=64)
-        out_codes = keep.tile([P, BLOCKS, T], U32, align_bytes=256)
-        out_scales = keep.tile([P, T], U8, align_bytes=256)
+        out_codes = keep.tile([P, BLOCKS, T], U32, align_bytes=4096)
+        out_scales = keep.tile([P, T], U8, align_bytes=4096)
 
         def cols(n):
             return slice(n * W, (n + 1) * W)

@@ -181,9 +181,10 @@ def tile_mix_aux_fm_pl_mul_kernel(tc, w, dy, v, e, g, out_0, out_1, out_2):
         last1 = interleave(on_vector, "rounded", result(2, 1))
         quantize_result(1, 0, rounded1[0])
         quantize_result(1, 1, rounded1[1])
+        store_codes(0, 2)
         quantize_result(2, 1, last1)
         quantize_result(2, 0, last0)
-        store_codes(0, 3)
+        store_codes(2, 3)
 
         scale_rows = out_2.bitcast(I32)
         for q in range(4):

@@ -16,8 +16,10 @@ E5M2 = mybir.dt.float8_e5m2_x4
 P = 128
 PACK = 4
 W = 512
-BLOCKS = M // W
+SLABS = M // W
 HALVES = T // W
+QUADRANT = 32
+DMA_ALIGN = 4096
 
 
 def tile_mix_aux_fm_pl_mul_kernel(tc, w, dy, v, e, g, out_0, out_1, out_2):
@@ -27,34 +29,30 @@ def tile_mix_aux_fm_pl_mul_kernel(tc, w, dy, v, e, g, out_0, out_1, out_2):
         stage = ctx.enter_context(tc.tile_pool(name="stage", bufs=4))
         psum = ctx.enter_context(tc.psum_pool(name="psum", bufs=1))
         ctx.enter_context(tc.manual_schedule())
-
-        def load(name, rows):
-            raw = keep.tile([P, PACK, rows.shape[1]], F32, name=name, align_bytes=4096)
-            nc.sync.dma_start(out=raw[:], in_=rows.rearrange("(p j) c -> p j c", j=PACK))
-            return raw
-
-        dy_raw = load("dy_raw", dy)
-        w_raw = load("w_raw", w)
-        e_raw = load("e_raw", e)
-        v_raw = load("v_raw", v)
-        gates = [load("g%d" % a, g[a * W : (a + 1) * W, :]) for a in range(BLOCKS)]
-
-        def result(a, h):
-            return gates[a][:, :, cols(h)]
-
-        dy_codes = keep.tile([P, T], U32, align_bytes=64)
-        dy_scales = keep.tile([P, T], U8, align_bytes=64)
-        e_codes = keep.tile([P, T], U32, align_bytes=64)
-        e_scales = keep.tile([P, T], U8, align_bytes=64)
-        w_codes = keep.tile([P, M], U32, align_bytes=64)
-        w_scales = keep.tile([P, M], U8, align_bytes=64)
-        v_codes = keep.tile([P, M], U32, align_bytes=64)
-        v_scales = keep.tile([P, M], U8, align_bytes=64)
-        out_codes = keep.tile([P, BLOCKS, T], U32, align_bytes=4096)
-        out_scales = keep.tile([P, T], U8, align_bytes=4096)
+        dma = nc.scalar.dma_start
+        on_vector, on_scalar = nc.vector.tensor_copy, nc.scalar.copy
 
         def cols(n):
             return slice(n * W, (n + 1) * W)
+
+        def load(name, rows):
+            raw = keep.tile([P, PACK, rows.shape[1]], F32, name=name, align_bytes=DMA_ALIGN)
+            dma(out=raw[:], in_=rows.rearrange("(p j) c -> p j c", j=PACK))
+            return raw
+
+        w_raw = load("w_raw", w)
+        v_raw = load("v_raw", v)
+        dy_raw = load("dy_raw", dy)
+        e_raw = load("e_raw", e)
+        slabs = [load("slab%d" % a, g[cols(a), :]) for a in range(SLABS)]
+
+        def planes(name, width):
+            codes = keep.tile([P, width], U32, name=name + "_codes", align_bytes=64)
+            scales = keep.tile([P, width], U8, name=name + "_scales", align_bytes=64)
+            return codes, scales
+
+        out_codes = keep.tile([P, SLABS, T], U32, align_bytes=DMA_ALIGN)
+        out_scales = keep.tile([P, T], U8, align_bytes=DMA_ALIGN)
 
         def interleave(copy, tag, raw):
             grouped = stage.tile([P, W * PACK], BF16, name=tag, align_bytes=64)
@@ -64,131 +62,92 @@ def tile_mix_aux_fm_pl_mul_kernel(tc, w, dy, v, e, g, out_0, out_1, out_2):
             )
             return grouped
 
-        def deal(copy, raw):
-            grouped = stage.tile([P, W * PACK], BF16, name="operand", align_bytes=64)
+        def deal(copy, tag, raw):
+            grouped = stage.tile([P, W * PACK], BF16, name=tag, align_bytes=64)
             copy(
                 out=grouped[:].rearrange("p (r m j) -> p m r j", r=PACK, j=PACK),
                 in_=raw.rearrange("p j (m r) -> p m r j", r=PACK),
             )
             return grouped
 
-        def quantize(grouped, codes, scales, fmt):
-            nc.vector.quantize_mx(out=codes.bitcast(fmt), scales=scales, in_=grouped[:])
+        def quantize_operand(name, raw, regroup, copies, fmt):
+            codes, scales = planes(name, W * len(copies))
+            grouped = [regroup(copy, "operand", raw[:, :, cols(n)]) for n, copy in enumerate(copies)]
+            vector_first = [n for n, copy in enumerate(copies) if copy is on_vector]
+            vector_first = vector_first + [n for n in range(len(copies)) if n not in vector_first]
+            for n in vector_first:
+                nc.vector.quantize_mx(out=codes[:, cols(n)].bitcast(fmt), scales=scales[:, cols(n)], in_=grouped[n][:])
+            return codes, scales, fmt
 
-        on_vector, on_scalar = nc.vector.tensor_copy, nc.scalar.copy
+        w_mx = quantize_operand("w", w_raw, deal, [on_vector, on_scalar, on_vector], E4M3)
+        v_mx = quantize_operand("v", v_raw, deal, [on_vector, on_scalar, on_vector], E4M3)
+        dy_mx = quantize_operand("dy", dy_raw, interleave, [on_vector, on_scalar], E5M2)
 
         banks = {}
 
-        def main_pass(a, h, r):
-            acc = psum.tile([P, W], F32, name="bank%d" % (h * PACK + r))
-            banks[(a, h, r)] = acc
+        def mx_pass(a, h, r, stationary, moving, first):
+            if first:
+                banks[(h, r)] = psum.tile([P, W], F32, name="bank%d" % (h * PACK + r))
             m_cols = slice(a * W + r * P, a * W + (r + 1) * P)
             nc.tensor.matmul_mx(
-                out=acc[:],
-                lhsT=w_codes[:, m_cols].bitcast(E4M3),
-                lhsT_scale=w_scales[:, m_cols],
-                rhs=dy_codes[:, cols(h)].bitcast(E5M2),
-                rhs_scale=dy_scales[:, cols(h)],
-                start=True,
-                stop=False,
-            )
-
-        def aux_pass(a, h, r):
-            m_cols = slice(a * W + r * P, a * W + (r + 1) * P)
-            nc.tensor.matmul_mx(
-                out=banks[(a, h, r)][:],
-                lhsT=v_codes[:, m_cols].bitcast(E4M3),
-                lhsT_scale=v_scales[:, m_cols],
-                rhs=e_codes[:, cols(h)].bitcast(E4M3),
-                rhs_scale=e_scales[:, cols(h)],
-                start=False,
-                stop=True,
+                out=banks[(h, r)][:],
+                lhsT=stationary[0][:, m_cols].bitcast(stationary[2]),
+                lhsT_scale=stationary[1][:, m_cols],
+                rhs=moving[0][:, cols(h)].bitcast(moving[2]),
+                rhs_scale=moving[1][:, cols(h)],
+                start=first,
+                stop=not first,
             )
 
         order = [(h, r) for h in range(HALVES) for r in range(PACK)]
-
-        def gate(a, h):
-            for r in range(PACK):
-                nc.vector.tensor_tensor(
-                    out=result(a, h)[:, r, :],
-                    in0=banks[(a, h, r)][:],
-                    in1=gates[a][:, r, cols(h)],
-                    op=mybir.AluOpType.mult,
-                )
-
-        def round_result(a):
-            return [interleave(on_scalar, "rounded", result(a, h)) for h in range(HALVES)]
+        for h, r in order:
+            mx_pass(0, h, r, w_mx, dy_mx, True)
+        e_mx = quantize_operand("e", e_raw, interleave, [on_vector, on_scalar], E4M3)
 
         def quantize_result(a, h, grouped):
-            quantize(grouped, out_codes[:, a, cols(h)], out_scales[4 * a : P, cols(h)], E4M3)
-
-        def store_result(a):
-            nc.sync.dma_start(out=out_0[cols(a), :].rearrange("(p j) c -> p j c", j=PACK), in_=gates[a][:])
+            nc.vector.quantize_mx(
+                out=out_codes[:, a, cols(h)].bitcast(E4M3), scales=out_scales[PACK * a : P, cols(h)], in_=grouped[:]
+            )
 
         def store_codes(first, last):
-            nc.sync.dma_start(
+            dma(
                 out=out_1[first:last].rearrange("a p t j -> p a (t j)").bitcast(I32),
                 in_=out_codes[:, first:last, :].bitcast(I32),
             )
 
-        dy0 = interleave(on_vector, "operand", dy_raw[:, :, cols(0)])
-        dy1 = interleave(on_scalar, "operand", dy_raw[:, :, cols(1)])
-        quantize(dy0, dy_codes[:, cols(0)], dy_scales[:, cols(0)], E5M2)
-        quantize(dy1, dy_codes[:, cols(1)], dy_scales[:, cols(1)], E5M2)
-        w0 = deal(on_vector, w_raw[:, :, cols(0)])
-        w1 = deal(on_scalar, w_raw[:, :, cols(1)])
-        w2 = deal(on_vector, w_raw[:, :, cols(2)])
-        quantize(w0, w_codes[:, cols(0)], w_scales[:, cols(0)], E4M3)
-        quantize(w2, w_codes[:, cols(2)], w_scales[:, cols(2)], E4M3)
-        quantize(w1, w_codes[:, cols(1)], w_scales[:, cols(1)], E4M3)
-        for h, r in order:
-            main_pass(0, h, r)
-        e0 = interleave(on_vector, "operand", e_raw[:, :, cols(0)])
-        e1 = interleave(on_scalar, "operand", e_raw[:, :, cols(1)])
-        quantize(e0, e_codes[:, cols(0)], e_scales[:, cols(0)], E4M3)
-        quantize(e1, e_codes[:, cols(1)], e_scales[:, cols(1)], E4M3)
-        v0 = deal(on_vector, v_raw[:, :, cols(0)])
-        v1 = deal(on_scalar, v_raw[:, :, cols(1)])
-        v2 = deal(on_vector, v_raw[:, :, cols(2)])
-        quantize(v0, v_codes[:, cols(0)], v_scales[:, cols(0)], E4M3)
-        quantize(v2, v_codes[:, cols(2)], v_scales[:, cols(2)], E4M3)
-        quantize(v1, v_codes[:, cols(1)], v_scales[:, cols(1)], E4M3)
+        rounded = {}
+        last = SLABS - 1
+        for a in range(SLABS):
+            for h, r in order:
+                if a > 0:
+                    mx_pass(a, h, r, w_mx, dy_mx, True)
+                mx_pass(a, h, r, v_mx, e_mx, False)
+            for h, r in order:
+                nc.vector.tensor_tensor(
+                    out=slabs[a][:, r, cols(h)],
+                    in0=banks[(h, r)][:],
+                    in1=slabs[a][:, r, cols(h)],
+                    op=mybir.AluOpType.mult,
+                )
+            dma(out=out_0[cols(a), :].rearrange("(p j) c -> p j c", j=PACK), in_=slabs[a][:])
+            if a < last:
+                for h in range(HALVES):
+                    rounded[(a, h)] = interleave(on_scalar, "rounded", slabs[a][:, :, cols(h)])
 
-        for h, r in order:
-            aux_pass(0, h, r)
-        gate(0, 0)
-        gate(0, 1)
-        store_result(0)
-        rounded0 = round_result(0)
-
-        for h, r in order:
-            main_pass(1, h, r)
-            aux_pass(1, h, r)
-        gate(1, 0)
-        gate(1, 1)
-        store_result(1)
-        rounded1 = round_result(1)
-
-        for h, r in order:
-            main_pass(2, h, r)
-            aux_pass(2, h, r)
-        gate(2, 0)
-        gate(2, 1)
-        store_result(2)
-        quantize_result(0, 0, rounded0[0])
-        quantize_result(0, 1, rounded0[1])
-        last0 = interleave(on_scalar, "rounded", result(2, 0))
-        last1 = interleave(on_vector, "rounded", result(2, 1))
-        quantize_result(1, 0, rounded1[0])
-        quantize_result(1, 1, rounded1[1])
-        store_codes(0, 2)
-        quantize_result(2, 1, last1)
-        quantize_result(2, 0, last0)
-        store_codes(2, 3)
+        for h in range(HALVES):
+            quantize_result(0, h, rounded[(0, h)])
+        rounded[(last, 0)] = interleave(on_scalar, "rounded", slabs[last][:, :, cols(0)])
+        rounded[(last, 1)] = interleave(on_vector, "rounded", slabs[last][:, :, cols(1)])
+        for h in range(HALVES):
+            quantize_result(1, h, rounded[(1, h)])
+        store_codes(0, last)
+        for h in (1, 0):
+            quantize_result(last, h, rounded[(last, h)])
+        store_codes(last, SLABS)
 
         scale_rows = out_2.bitcast(I32)
-        for q in range(4):
-            nc.sync.dma_start(
-                out=scale_rows[:, 4 * q : 4 * q + 4, :],
-                in_=out_scales[32 * q : 32 * q + 4 * BLOCKS, :].bitcast(I32),
+        for q in range(P // QUADRANT):
+            dma(
+                out=scale_rows[:, PACK * q : PACK * (q + 1), :],
+                in_=out_scales[QUADRANT * q : QUADRANT * q + PACK * SLABS, :].bitcast(I32),
             )

@@ -52,7 +52,7 @@ def tile_mix_aux_fm_pl_mul_kernel(tc, w, dy, v, e, g, out_0, out_1, out_2):
             return codes, scales
 
         out_codes = keep.tile([P, SLABS, T], U32, align_bytes=DMA_ALIGN)
-        out_scales = keep.tile([P, T], U8, align_bytes=DMA_ALIGN)
+        out_scales = keep.tile([P, SLABS, T], U8, align_bytes=DMA_ALIGN)
 
         def interleave(copy, tag, raw):
             grouped = stage.tile([P, W * PACK], BF16, name=tag, align_bytes=64)
@@ -106,7 +106,7 @@ def tile_mix_aux_fm_pl_mul_kernel(tc, w, dy, v, e, g, out_0, out_1, out_2):
 
         def quantize_result(a, h, grouped):
             nc.vector.quantize_mx(
-                out=out_codes[:, a, cols(h)].bitcast(E4M3), scales=out_scales[PACK * a : P, cols(h)], in_=grouped[:]
+                out=out_codes[:, a, cols(h)].bitcast(E4M3), scales=out_scales[:, a, cols(h)], in_=grouped[:]
             )
 
         def store_codes(first, last):
@@ -145,9 +145,6 @@ def tile_mix_aux_fm_pl_mul_kernel(tc, w, dy, v, e, g, out_0, out_1, out_2):
             quantize_result(last, h, rounded[(last, h)])
         store_codes(last, SLABS)
 
-        scale_rows = out_2.bitcast(I32)
-        for q in range(P // QUADRANT):
-            dma(
-                out=scale_rows[:, PACK * q : PACK * (q + 1), :],
-                in_=out_scales[QUADRANT * q : QUADRANT * q + PACK * SLABS, :].bitcast(I32),
-            )
+        scale_rows = out_2.bitcast(I32).rearrange("a (q r) t -> r q a t", r=PACK)
+        for r in range(PACK):
+            dma(out=scale_rows[r], in_=out_scales[r:P:QUADRANT, :, :].bitcast(I32))

@@ -140,10 +140,9 @@ def tile_mix_aux_fm_pl_mul_kernel(tc, w, dy, v, e, g, out_0, out_1, out_2):
         rounded[(last, 1)] = interleave(on_vector, "rounded", slabs[last][:, :, cols(1)])
         for h in range(HALVES):
             quantize_result(1, h, rounded[(1, h)])
-        store_codes(0, last)
         for h in (1, 0):
             quantize_result(last, h, rounded[(last, h)])
-        store_codes(last, SLABS)
+        store_codes(0, SLABS)
 
         scale_rows = out_2.bitcast(I32).rearrange("a (q r) t -> r q a t", r=PACK)
         for r in range(PACK):

@@ -20,130 +20,116 @@ SLABS = M // W
 HALVES = T // W
 QUADRANT = 32
 DMA_ALIGN = 4096
+MX_ALIGN = 64
+STAGE_BUFS = 4
 
 
 def tile_mix_aux_fm_pl_mul_kernel(tc, w, dy, v, e, g, out_0, out_1, out_2):
     nc = tc.nc
     with ExitStack() as ctx:
         keep = ctx.enter_context(tc.tile_pool(name="keep", bufs=1))
-        stage = ctx.enter_context(tc.tile_pool(name="stage", bufs=4))
+        stage = ctx.enter_context(tc.tile_pool(name="stage", bufs=STAGE_BUFS))
         psum = ctx.enter_context(tc.psum_pool(name="psum", bufs=1))
         ctx.enter_context(tc.manual_schedule())
-        dma = nc.scalar.dma_start
         on_vector, on_scalar = nc.vector.tensor_copy, nc.scalar.copy
 
-        def cols(n):
+        def piece(n):
             return slice(n * W, (n + 1) * W)
 
-        def load(name, rows):
-            raw = keep.tile([P, PACK, rows.shape[1]], F32, name=name, align_bytes=DMA_ALIGN)
-            dma(out=raw[:], in_=rows.rearrange("(p j) c -> p j c", j=PACK))
-            return raw
+        def by_partition(rows):
+            return rows.rearrange("(p j) c -> p j c", j=PACK)
 
-        w_raw = load("w_raw", w)
-        v_raw = load("v_raw", v)
-        dy_raw = load("dy_raw", dy)
-        e_raw = load("e_raw", e)
-        slabs = [load("slab%d" % a, g[cols(a), :]) for a in range(SLABS)]
-
-        def planes(name, width):
-            codes = keep.tile([P, width], U32, name=name + "_codes", align_bytes=64)
-            scales = keep.tile([P, width], U8, name=name + "_scales", align_bytes=64)
-            return codes, scales
+        sources = [("w", w), ("v", v), ("dy", dy), ("e", e)]
+        sources = sources + [("slab%d" % a, g[piece(a), :]) for a in range(SLABS)]
+        raw = {}
+        for name, rows in sources:
+            raw[name] = keep.tile([P, PACK, rows.shape[1]], F32, name=name + "_raw", align_bytes=DMA_ALIGN)
+            nc.sync.dma_start(out=raw[name][:], in_=by_partition(rows))
+        slabs = [raw["slab%d" % a] for a in range(SLABS)]
 
         out_codes = keep.tile([P, SLABS, T], U32, align_bytes=DMA_ALIGN)
         out_scales = keep.tile([P, SLABS, T], U8, align_bytes=DMA_ALIGN)
 
-        def interleave(copy, tag, raw):
-            grouped = stage.tile([P, W * PACK], BF16, name=tag, align_bytes=64)
-            copy(
-                out=grouped[:].rearrange("p (c i j) -> p c j i", i=4, j=PACK),
-                in_=raw.rearrange("p j (c i) -> p c j i", i=4),
-            )
+        def rounded(copy, tag, source, dealt):
+            grouped = stage.tile([P, W * PACK], BF16, name=tag, align_bytes=MX_ALIGN)
+            if dealt:
+                out = grouped[:].rearrange("p (r m j) -> p m r j", r=PACK, j=PACK)
+                in_ = source.rearrange("p j (m r) -> p m r j", r=PACK)
+            else:
+                out = grouped[:].rearrange("p (c i j) -> p c j i", i=4, j=PACK)
+                in_ = source.rearrange("p j (c i) -> p c j i", i=4)
+            copy(out=out, in_=in_)
             return grouped
 
-        def deal(copy, tag, raw):
-            grouped = stage.tile([P, W * PACK], BF16, name=tag, align_bytes=64)
-            copy(
-                out=grouped[:].rearrange("p (r m j) -> p m r j", r=PACK, j=PACK),
-                in_=raw.rearrange("p j (m r) -> p m r j", r=PACK),
-            )
-            return grouped
-
-        def quantize_operand(name, raw, regroup, copies, fmt):
-            codes, scales = planes(name, W * len(copies))
-            grouped = [regroup(copy, "operand", raw[:, :, cols(n)]) for n, copy in enumerate(copies)]
-            vector_first = [n for n, copy in enumerate(copies) if copy is on_vector]
-            vector_first = vector_first + [n for n in range(len(copies)) if n not in vector_first]
-            for n in vector_first:
-                nc.vector.quantize_mx(out=codes[:, cols(n)].bitcast(fmt), scales=scales[:, cols(n)], in_=grouped[n][:])
+        def operand(name, fmt, dealt):
+            pieces = raw[name].shape[2] // W
+            codes = keep.tile([P, pieces * W], U32, name=name + "_codes", align_bytes=MX_ALIGN)
+            scales = keep.tile([P, pieces * W], U8, name=name + "_scales", align_bytes=MX_ALIGN)
+            grouped = [
+                rounded(on_scalar if n == 1 else on_vector, "operand", raw[name][:, :, piece(n)], dealt)
+                for n in range(pieces)
+            ]
+            for n in [n for n in range(pieces) if n != 1] + [1]:
+                nc.vector.quantize_mx(out=codes[:, piece(n)].bitcast(fmt), scales=scales[:, piece(n)], in_=grouped[n][:])
             return codes, scales, fmt
 
-        w_mx = quantize_operand("w", w_raw, deal, [on_vector, on_scalar, on_vector], E4M3)
-        v_mx = quantize_operand("v", v_raw, deal, [on_vector, on_scalar, on_vector], E4M3)
-        dy_mx = quantize_operand("dy", dy_raw, interleave, [on_vector, on_scalar], E5M2)
-
         banks = {}
+        bank_order = [(h, j) for h in range(HALVES) for j in range(PACK)]
 
-        def mx_pass(a, h, r, stationary, moving, first):
+        def mx_pass(a, h, j, stationary, moving, first):
             if first:
-                banks[(h, r)] = psum.tile([P, W], F32, name="bank%d" % (h * PACK + r))
-            m_cols = slice(a * W + r * P, a * W + (r + 1) * P)
+                banks[(h, j)] = psum.tile([P, W], F32, name="bank%d" % (h * PACK + j))
+            places = slice(a * W + j * P, a * W + (j + 1) * P)
             nc.tensor.matmul_mx(
-                out=banks[(h, r)][:],
-                lhsT=stationary[0][:, m_cols].bitcast(stationary[2]),
-                lhsT_scale=stationary[1][:, m_cols],
-                rhs=moving[0][:, cols(h)].bitcast(moving[2]),
-                rhs_scale=moving[1][:, cols(h)],
+                out=banks[(h, j)][:],
+                lhsT=stationary[0][:, places].bitcast(stationary[2]),
+                lhsT_scale=stationary[1][:, places],
+                rhs=moving[0][:, piece(h)].bitcast(moving[2]),
+                rhs_scale=moving[1][:, piece(h)],
                 start=first,
                 stop=not first,
             )
 
-        order = [(h, r) for h in range(HALVES) for r in range(PACK)]
-        for h, r in order:
-            mx_pass(0, h, r, w_mx, dy_mx, True)
-        e_mx = quantize_operand("e", e_raw, interleave, [on_vector, on_scalar], E4M3)
+        w_mx = operand("w", E4M3, True)
+        v_mx = operand("v", E4M3, True)
+        dy_mx = operand("dy", E5M2, False)
+        for h, j in bank_order:
+            mx_pass(0, h, j, w_mx, dy_mx, True)
+        e_mx = operand("e", E4M3, False)
 
-        def quantize_result(a, h, grouped):
-            nc.vector.quantize_mx(
-                out=out_codes[:, a, cols(h)].bitcast(E4M3), scales=out_scales[:, a, cols(h)], in_=grouped[:]
-            )
-
-        def store_codes(first, last):
-            dma(
-                out=out_1[first:last].rearrange("a p t j -> p a (t j)").bitcast(I32),
-                in_=out_codes[:, first:last, :].bitcast(I32),
-            )
-
-        rounded = {}
+        result = {}
         last = SLABS - 1
         for a in range(SLABS):
-            for h, r in order:
+            for h, j in bank_order:
                 if a > 0:
-                    mx_pass(a, h, r, w_mx, dy_mx, True)
-                mx_pass(a, h, r, v_mx, e_mx, False)
-            for h, r in order:
-                nc.vector.tensor_tensor(
-                    out=slabs[a][:, r, cols(h)],
-                    in0=banks[(h, r)][:],
-                    in1=slabs[a][:, r, cols(h)],
-                    op=mybir.AluOpType.mult,
-                )
-            dma(out=out_0[cols(a), :].rearrange("(p j) c -> p j c", j=PACK), in_=slabs[a][:])
+                    mx_pass(a, h, j, w_mx, dy_mx, True)
+                mx_pass(a, h, j, v_mx, e_mx, False)
+            for h, j in bank_order:
+                in_place = slabs[a][:, j, piece(h)]
+                nc.vector.tensor_tensor(out=in_place, in0=banks[(h, j)][:], in1=in_place, op=mybir.AluOpType.mult)
+            nc.scalar.dma_start(out=by_partition(out_0[piece(a), :]), in_=slabs[a][:])
             if a < last:
                 for h in range(HALVES):
-                    rounded[(a, h)] = interleave(on_scalar, "rounded", slabs[a][:, :, cols(h)])
+                    result[(a, h)] = rounded(on_scalar, "result", slabs[a][:, :, piece(h)], False)
+
+        def quantize_result(a, h):
+            nc.vector.quantize_mx(
+                out=out_codes[:, a, piece(h)].bitcast(E4M3), scales=out_scales[:, a, piece(h)], in_=result[(a, h)][:]
+            )
 
         for h in range(HALVES):
-            quantize_result(0, h, rounded[(0, h)])
-        rounded[(last, 0)] = interleave(on_scalar, "rounded", slabs[last][:, :, cols(0)])
-        rounded[(last, 1)] = interleave(on_vector, "rounded", slabs[last][:, :, cols(1)])
+            quantize_result(0, h)
+        result[(last, 0)] = rounded(on_scalar, "result", slabs[last][:, :, piece(0)], False)
+        result[(last, 1)] = rounded(on_vector, "result", slabs[last][:, :, piece(1)], False)
         for h in range(HALVES):
-            quantize_result(1, h, rounded[(1, h)])
+            quantize_result(1, h)
         for h in (1, 0):
-            quantize_result(last, h, rounded[(last, h)])
-        store_codes(0, SLABS)
+            quantize_result(last, h)
 
+        nc.scalar.dma_start(
+            out=out_1.rearrange("a p t j -> p a (t j)").bitcast(I32),
+            in_=out_codes[:].bitcast(I32),
+        )
         scale_rows = out_2.bitcast(I32).rearrange("a (q r) t -> r q a t", r=PACK)
         for r in range(PACK):
-            dma(out=scale_rows[r], in_=out_scales[r:P:QUADRANT, :, :].bitcast(I32))
+            nc.scalar.dma_start(out=scale_rows[r], in_=out_scales[r:P:QUADRANT, :, :].bitcast(I32))

@@ -98,6 +98,7 @@ def tile_mix_aux_fm_pl_mul_kernel(tc, w, dy, v, e, g, out_0, out_1, out_2):
         e_mx = operand("e", E4M3, False)
 
         result = {}
+        queues = [nc.scalar, nc.sync]
         last = SLABS - 1
         for a in range(SLABS):
             for h, j in bank_order:
@@ -107,7 +108,7 @@ def tile_mix_aux_fm_pl_mul_kernel(tc, w, dy, v, e, g, out_0, out_1, out_2):
             for h, j in bank_order:
                 in_place = slabs[a][:, j, piece(h)]
                 nc.vector.tensor_tensor(out=in_place, in0=banks[(h, j)][:], in1=in_place, op=mybir.AluOpType.mult)
-            nc.scalar.dma_start(out=by_partition(out_0[piece(a), :]), in_=slabs[a][:])
+            queues[a % 2].dma_start(out=by_partition(out_0[piece(a), :]), in_=slabs[a][:])
             if a < last:
                 for h in range(HALVES):
                     result[(a, h)] = rounded(on_scalar, "result", slabs[a][:, :, piece(h)], False)
@@ -126,7 +127,7 @@ def tile_mix_aux_fm_pl_mul_kernel(tc, w, dy, v, e, g, out_0, out_1, out_2):
         for h in (1, 0):
             quantize_result(last, h)
 
-        nc.scalar.dma_start(
+        queues[SLABS % 2].dma_start(
             out=out_1.rearrange("a p t j -> p a (t j)").bitcast(I32),
             in_=out_codes[:].bitcast(I32),
         )

@@ -133,4 +133,4 @@ def tile_mix_aux_fm_pl_mul_kernel(tc, w, dy, v, e, g, out_0, out_1, out_2):
         )
         scale_rows = out_2.bitcast(I32).rearrange("a (q r) t -> r q a t", r=PACK)
         for r in range(PACK):
-            nc.scalar.dma_start(out=scale_rows[r], in_=out_scales[r:P:QUADRANT, :, :].bitcast(I32))
+            queues[SLABS % 2].dma_start(out=scale_rows[r], in_=out_scales[r:P:QUADRANT, :, :].bitcast(I32))

@@ -18,114 +18,155 @@ PACK = 4
 W = 512
 SLABS = M // W
 HALVES = T // W
+BANKS = PACK * HALVES
+WIDE = 1024
 QUADRANT = 32
 DMA_ALIGN = 4096
 MX_ALIGN = 64
-STAGE_BUFS = 4
+E_ON_VECTOR = 640
+COPIED = 4
 
 
 def tile_mix_aux_fm_pl_mul_kernel(tc, w, dy, v, e, g, out_0, out_1, out_2):
     nc = tc.nc
     with ExitStack() as ctx:
+        moved = ctx.enter_context(tc.tile_pool(name="moved", bufs=1))
         keep = ctx.enter_context(tc.tile_pool(name="keep", bufs=1))
-        stage = ctx.enter_context(tc.tile_pool(name="stage", bufs=STAGE_BUFS))
         psum = ctx.enter_context(tc.psum_pool(name="psum", bufs=1))
         ctx.enter_context(tc.manual_schedule())
         on_vector, on_scalar = nc.vector.tensor_copy, nc.scalar.copy
 
-        def piece(n):
-            return slice(n * W, (n + 1) * W)
+        def span(first, count, width):
+            return slice(first * width, (first + count) * width)
 
         def by_partition(rows):
             return rows.rearrange("(p j) c -> p j c", j=PACK)
 
-        sources = [("w", w), ("v", v), ("dy", dy), ("e", e)]
-        sources = sources + [("slab%d" % a, g[piece(a), :]) for a in range(SLABS)]
+        sources = [("dy", dy), ("w", w), ("v", v), ("e", e)]
+        sources = sources + [("slab%d" % a, g[span(a, 1, W), :]) for a in range(SLABS)]
         raw = {}
+        used = 0
         for name, rows in sources:
-            raw[name] = keep.tile([P, PACK, rows.shape[1]], F32, name=name + "_raw", align_bytes=DMA_ALIGN)
+            raw[name] = moved.tile([P, PACK, rows.shape[1]], F32, name=name + "_raw", align_bytes=DMA_ALIGN, offset=used)
+            used = used + PACK * rows.shape[1] * 4
             nc.sync.dma_start(out=raw[name][:], in_=by_partition(rows))
         slabs = [raw["slab%d" % a] for a in range(SLABS)]
 
-        out_codes = keep.tile([P, SLABS, T], U32, align_bytes=DMA_ALIGN)
-        out_scales = keep.tile([P, SLABS, T], U8, align_bytes=DMA_ALIGN)
+        out_codes = moved.tile([P, SLABS, T], U32, align_bytes=DMA_ALIGN, offset=used)
+        out_scales = moved.tile([P, SLABS, T], U8, align_bytes=DMA_ALIGN, offset=used + SLABS * T * 4)
 
-        def rounded(copy, tag, source, dealt):
-            grouped = stage.tile([P, W * PACK], BF16, name=tag, align_bytes=MX_ALIGN)
-            if dealt:
-                out = grouped[:].rearrange("p (r m j) -> p m r j", r=PACK, j=PACK)
-                in_ = source.rearrange("p j (m r) -> p m r j", r=PACK)
-            else:
-                out = grouped[:].rearrange("p (c i j) -> p c j i", i=4, j=PACK)
-                in_ = source.rearrange("p j (c i) -> p c j i", i=4)
-            copy(out=out, in_=in_)
-            return grouped
+        def deal(copy, grouped, source):
+            copy(
+                out=grouped.rearrange("p (a r m j) -> p a m r j", r=PACK, m=P, j=PACK),
+                in_=source.rearrange("p j (a m r) -> p a m r j", m=P, r=PACK),
+            )
 
-        def operand(name, fmt, dealt):
-            pieces = raw[name].shape[2] // W
-            codes = keep.tile([P, pieces * W], U32, name=name + "_codes", align_bytes=MX_ALIGN)
-            scales = keep.tile([P, pieces * W], U8, name=name + "_scales", align_bytes=MX_ALIGN)
-            grouped = [
-                rounded(on_scalar if n == 1 else on_vector, "operand", raw[name][:, :, piece(n)], dealt)
-                for n in range(pieces)
-            ]
-            for n in [n for n in range(pieces) if n != 1] + [1]:
-                nc.vector.quantize_mx(out=codes[:, piece(n)].bitcast(fmt), scales=scales[:, piece(n)], in_=grouped[n][:])
-            return codes, scales, fmt
+        def interleave(copy, grouped, source):
+            copy(
+                out=grouped.rearrange("p (c i j) -> p c j i", i=4, j=PACK),
+                in_=source.rearrange("p j (c i) -> p c j i", i=4),
+            )
+
+        w_slot = [SLABS - 1] + list(range(SLABS - 1))
+        weights_bf = keep.tile([P, 2 * M * PACK], BF16, name="wide_bf", align_bytes=MX_ALIGN)
+        weight_codes = keep.tile([P, 2 * M], U32, align_bytes=MX_ALIGN)
+        weight_scales = keep.tile([P, 2 * M], U8, align_bytes=MX_ALIGN)
+        moving = {}
+        for name, fmt in (("dy", E5M2), ("e", E4M3)):
+            moving[name] = (
+                keep.tile([P, T * PACK], BF16, name=name + "_bf", align_bytes=MX_ALIGN),
+                keep.tile([P, T], U32, name=name + "_codes", align_bytes=MX_ALIGN),
+                keep.tile([P, T], U8, name=name + "_scales", align_bytes=MX_ALIGN),
+                fmt,
+            )
+
+        def quantize_weights(n):
+            nc.vector.quantize_mx(
+                out=weight_codes[:, span(n, 1, WIDE)].bitcast(E4M3),
+                scales=weight_scales[:, span(n, 1, WIDE)],
+                in_=weights_bf[:, span(n, 1, WIDE * PACK)],
+            )
+
+        def quantize_moving(name):
+            grouped, codes, scales, fmt = moving[name]
+            nc.vector.quantize_mx(out=codes[:].bitcast(fmt), scales=scales[:], in_=grouped[:])
+
+        interleave(on_scalar, moving["dy"][0][:], raw["dy"][:])
+        deal(on_scalar, weights_bf[:, span(w_slot[1], SLABS - 1, W * PACK)], raw["w"][:, :, span(1, SLABS - 1, W)])
+        deal(on_scalar, weights_bf[:, span(w_slot[0], 1, W * PACK)], raw["w"][:, :, span(0, 1, W)])
+        deal(on_scalar, weights_bf[:, span(SLABS, 1, W * PACK)], raw["v"][:, :, span(0, 1, W)])
+        interleave(on_scalar, moving["e"][0][:, E_ON_VECTOR * PACK :], raw["e"][:, :, E_ON_VECTOR:])
+        quantize_moving("dy")
+        quantize_weights(0)
+        deal(on_vector, weights_bf[:, span(SLABS + 1, SLABS - 1, W * PACK)], raw["v"][:, :, span(1, SLABS - 1, W)])
+        quantize_weights(1)
+        quantize_weights(2)
+        interleave(on_vector, moving["e"][0][:, : E_ON_VECTOR * PACK], raw["e"][:, :, :E_ON_VECTOR])
+        quantize_moving("e")
 
         banks = {}
-        bank_order = [(h, j) for h in range(HALVES) for j in range(PACK)]
+        direct = BANKS - COPIED
+        bank_order = [b for pair in zip(range(direct, BANKS), range(direct)) for b in pair]
 
-        def mx_pass(a, h, j, stationary, moving, first):
+        def mx_pass(a, b, first):
             if first:
-                banks[(h, j)] = psum.tile([P, W], F32, name="bank%d" % (h * PACK + j))
-            places = slice(a * W + j * P, a * W + (j + 1) * P)
+                banks[b] = psum.tile([P, W], F32, name="bank%d" % b)
+            j, h = divmod(b, HALVES)
+            places = span((w_slot[a] if first else SLABS + a) * PACK + j, 1, P)
+            codes, scales, fmt = moving["dy" if first else "e"][1:]
             nc.tensor.matmul_mx(
-                out=banks[(h, j)][:],
-                lhsT=stationary[0][:, places].bitcast(stationary[2]),
-                lhsT_scale=stationary[1][:, places],
-                rhs=moving[0][:, piece(h)].bitcast(moving[2]),
-                rhs_scale=moving[1][:, piece(h)],
+                out=banks[b][:],
+                lhsT=weight_codes[:, places].bitcast(E4M3),
+                lhsT_scale=weight_scales[:, places],
+                rhs=codes[:, span(h, 1, W)].bitcast(fmt),
+                rhs_scale=scales[:, span(h, 1, W)],
                 start=first,
                 stop=not first,
             )
 
-        w_mx = operand("w", E4M3, True)
-        v_mx = operand("v", E4M3, True)
-        dy_mx = operand("dy", E5M2, False)
-        for h, j in bank_order:
-            mx_pass(0, h, j, w_mx, dy_mx, True)
-        e_mx = operand("e", E4M3, False)
+        def multiply(in_place, sums):
+            nc.vector.tensor_tensor(out=in_place, in0=sums, in1=in_place, op=mybir.AluOpType.mult)
 
-        result = {}
+        for b in bank_order:
+            mx_pass(0, b, True)
+
+        result_bf = keep.tile([P, SLABS * T * PACK], BF16, name="wide_bf", align_bytes=MX_ALIGN)
+        copied = keep.tile([P, COPIED * W], F32)
+
+        def round_result(copy, a, h):
+            interleave(copy, result_bf[:, span(a * HALVES + h, 1, W * PACK)], slabs[a][:, :, span(h, 1, W)])
+
         queues = [nc.scalar, nc.sync]
         last = SLABS - 1
         for a in range(SLABS):
-            for h, j in bank_order:
+            flat = slabs[a][:].rearrange("p j t -> p (j t)")
+            for b in bank_order:
                 if a > 0:
-                    mx_pass(a, h, j, w_mx, dy_mx, True)
-                mx_pass(a, h, j, v_mx, e_mx, False)
-            for h, j in bank_order:
-                in_place = slabs[a][:, j, piece(h)]
-                nc.vector.tensor_tensor(out=in_place, in0=banks[(h, j)][:], in1=in_place, op=mybir.AluOpType.mult)
-            queues[a % 2].dma_start(out=by_partition(out_0[piece(a), :]), in_=slabs[a][:])
+                    mx_pass(a, b, True)
+                mx_pass(a, b, False)
+            if a == 0:
+                for b in range(direct, BANKS):
+                    on_scalar(out=copied[:, span(b - direct, 1, W)], in_=banks[b][:])
+                for b in range(direct):
+                    multiply(flat[:, span(b, 1, W)], banks[b][:])
+                multiply(flat[:, span(direct, COPIED, W)], copied[:])
+            else:
+                for b in bank_order:
+                    multiply(flat[:, span(b, 1, W)], banks[b][:])
+            queues[a % 2].dma_start(out=by_partition(out_0[span(a, 1, W), :]), in_=slabs[a][:])
             if a < last:
-                for h in range(HALVES):
-                    result[(a, h)] = rounded(on_scalar, "result", slabs[a][:, :, piece(h)], False)
+                interleave(on_scalar, result_bf[:, span(a, 1, T * PACK)], slabs[a][:])
 
-        def quantize_result(a, h):
+        def quantize_result(a):
             nc.vector.quantize_mx(
-                out=out_codes[:, a, piece(h)].bitcast(E4M3), scales=out_scales[:, a, piece(h)], in_=result[(a, h)][:]
+                out=out_codes[:, a, :].bitcast(E4M3), scales=out_scales[:, a, :], in_=result_bf[:, span(a, 1, T * PACK)]
             )
 
-        for h in range(HALVES):
-            quantize_result(0, h)
-        result[(last, 0)] = rounded(on_scalar, "result", slabs[last][:, :, piece(0)], False)
-        result[(last, 1)] = rounded(on_vector, "result", slabs[last][:, :, piece(1)], False)
-        for h in range(HALVES):
-            quantize_result(1, h)
-        for h in (1, 0):
-            quantize_result(last, h)
+        quantize_result(0)
+        round_result(on_scalar, last, 0)
+        round_result(on_vector, last, 1)
+        quantize_result(1)
+        quantize_result(last)
 
         queues[SLABS % 2].dma_start(
             out=out_1.rearrange("a p t j -> p a (t j)").bitcast(I32),

@@ -92,11 +92,11 @@ def tile_mix_aux_fm_pl_mul_kernel(tc, w, dy, v, e, g, out_0, out_1, out_2):
             nc.vector.quantize_mx(out=codes[:].bitcast(fmt), scales=scales[:], in_=grouped[:])
 
         interleave(on_scalar, moving["dy"][0][:], raw["dy"][:])
-        deal(on_scalar, weights_bf[:, span(w_slot[1], SLABS - 1, W * PACK)], raw["w"][:, :, span(1, SLABS - 1, W)])
         deal(on_scalar, weights_bf[:, span(w_slot[0], 1, W * PACK)], raw["w"][:, :, span(0, 1, W)])
         deal(on_scalar, weights_bf[:, span(SLABS, 1, W * PACK)], raw["v"][:, :, span(0, 1, W)])
         interleave(on_scalar, moving["e"][0][:, E_ON_VECTOR * PACK :], raw["e"][:, :, E_ON_VECTOR:])
         quantize_moving("dy")
+        deal(on_vector, weights_bf[:, span(w_slot[1], SLABS - 1, W * PACK)], raw["w"][:, :, span(1, SLABS - 1, W)])
         quantize_weights(0)
         deal(on_vector, weights_bf[:, span(SLABS + 1, SLABS - 1, W * PACK)], raw["v"][:, :, span(1, SLABS - 1, W)])
         quantize_weights(1)
@@ -133,10 +133,6 @@ def tile_mix_aux_fm_pl_mul_kernel(tc, w, dy, v, e, g, out_0, out_1, out_2):
         result_bf = keep.tile([P, SLABS * T * PACK], BF16, name="wide_bf", align_bytes=MX_ALIGN)
         copied = keep.tile([P, COPIED * W], F32)
 
-        def round_result(copy, a, h):
-            interleave(copy, result_bf[:, span(a * HALVES + h, 1, W * PACK)], slabs[a][:, :, span(h, 1, W)])
-
-        queues = [nc.scalar, nc.sync]
         last = SLABS - 1
         for a in range(SLABS):
             flat = slabs[a][:].rearrange("p j t -> p (j t)")
@@ -153,7 +149,7 @@ def tile_mix_aux_fm_pl_mul_kernel(tc, w, dy, v, e, g, out_0, out_1, out_2):
             else:
                 for b in bank_order:
                     multiply(flat[:, span(b, 1, W)], banks[b][:])
-            queues[a % 2].dma_start(out=by_partition(out_0[span(a, 1, W), :]), in_=slabs[a][:])
+            nc.sync.dma_start(out=by_partition(out_0[span(a, 1, W), :]), in_=slabs[a][:])
             if a < last:
                 interleave(on_scalar, result_bf[:, span(a, 1, T * PACK)], slabs[a][:])
 
@@ -162,16 +158,19 @@ def tile_mix_aux_fm_pl_mul_kernel(tc, w, dy, v, e, g, out_0, out_1, out_2):
                 out=out_codes[:, a, :].bitcast(E4M3), scales=out_scales[:, a, :], in_=result_bf[:, span(a, 1, T * PACK)]
             )
 
-        quantize_result(0)
-        round_result(on_scalar, last, 0)
-        round_result(on_vector, last, 1)
-        quantize_result(1)
-        quantize_result(last)
+        def store_codes(first, count):
+            nc.sync.dma_start(
+                out=out_1[span(first, count, 1)].rearrange("a p t j -> p a (t j)").bitcast(I32),
+                in_=out_codes[:, span(first, count, 1), :].bitcast(I32),
+            )
 
-        queues[SLABS % 2].dma_start(
-            out=out_1.rearrange("a p t j -> p a (t j)").bitcast(I32),
-            in_=out_codes[:].bitcast(I32),
-        )
+        quantize_result(0)
+        interleave(on_vector, result_bf[:, span(last, 1, T * PACK)], slabs[last][:])
+        quantize_result(1)
+        store_codes(0, last)
+        quantize_result(last)
+        store_codes(last, 1)
+
         scale_rows = out_2.bitcast(I32).rearrange("a (q r) t -> r q a t", r=PACK)
         for r in range(PACK):
-            queues[SLABS % 2].dma_start(out=scale_rows[r], in_=out_scales[r:P:QUADRANT, :, :].bitcast(I32))
+            nc.sync.dma_start(out=scale_rows[r], in_=out_scales[r:P:QUADRANT, :, :].bitcast(I32))

from contextlib import ExitStack

import concourse.mybir as mybir

K, M, T = 512, 1536, 1024
FLOPS = 2 * 2 * K * M * T

F32 = mybir.dt.float32
BF16 = mybir.dt.bfloat16
U32 = mybir.dt.uint32
I32 = mybir.dt.int32
U8 = mybir.dt.uint8
E4M3 = mybir.dt.float8_e4m3fn_x4
E5M2 = mybir.dt.float8_e5m2_x4

P = 128
PACK = 4
W = 512
SLABS = M // W
HALVES = T // W
BANKS = PACK * HALVES
WIDE = 1024
QUADRANT = 32
DMA_ALIGN = 4096
MX_ALIGN = 64
E_ON_VECTOR = 640
COPIED = 4


def tile_mix_aux_fm_pl_mul_kernel(tc, w, dy, v, e, g, out_0, out_1, out_2):
    nc = tc.nc
    with ExitStack() as ctx:
        moved = ctx.enter_context(tc.tile_pool(name="moved", bufs=1))
        keep = ctx.enter_context(tc.tile_pool(name="keep", bufs=1))
        psum = ctx.enter_context(tc.psum_pool(name="psum", bufs=1))
        ctx.enter_context(tc.manual_schedule())
        on_vector, on_scalar = nc.vector.tensor_copy, nc.scalar.copy

        def span(first, count, width):
            return slice(first * width, (first + count) * width)

        def by_partition(rows):
            return rows.rearrange("(p j) c -> p j c", j=PACK)

        sources = [("dy", dy), ("w", w), ("v", v), ("e", e)]
        sources = sources + [("slab%d" % a, g[span(a, 1, W), :]) for a in range(SLABS)]
        raw = {}
        used = 0
        for name, rows in sources:
            raw[name] = moved.tile([P, PACK, rows.shape[1]], F32, name=name + "_raw", align_bytes=DMA_ALIGN, offset=used)
            used = used + PACK * rows.shape[1] * 4
            nc.sync.dma_start(out=raw[name][:], in_=by_partition(rows))
        slabs = [raw["slab%d" % a] for a in range(SLABS)]

        out_codes = moved.tile([P, SLABS, T], U32, align_bytes=DMA_ALIGN, offset=used)
        out_scales = moved.tile([P, SLABS, T], U8, align_bytes=DMA_ALIGN, offset=used + SLABS * T * 4)

        def deal(copy, grouped, source):
            copy(
                out=grouped.rearrange("p (a r m j) -> p a m r j", r=PACK, m=P, j=PACK),
                in_=source.rearrange("p j (a m r) -> p a m r j", m=P, r=PACK),
            )

        def interleave(copy, grouped, source):
            copy(
                out=grouped.rearrange("p (c i j) -> p c j i", i=4, j=PACK),
                in_=source.rearrange("p j (c i) -> p c j i", i=4),
            )

        w_slot = [SLABS - 1] + list(range(SLABS - 1))
        weights_bf = keep.tile([P, 2 * M * PACK], BF16, name="wide_bf", align_bytes=MX_ALIGN)
        weight_codes = keep.tile([P, 2 * M], U32, align_bytes=MX_ALIGN)
        weight_scales = keep.tile([P, 2 * M], U8, align_bytes=MX_ALIGN)
        moving = {}
        for name, fmt in (("dy", E5M2), ("e", E4M3)):
            moving[name] = (
                keep.tile([P, T * PACK], BF16, name=name + "_bf", align_bytes=MX_ALIGN),
                keep.tile([P, T], U32, name=name + "_codes", align_bytes=MX_ALIGN),
                keep.tile([P, T], U8, name=name + "_scales", align_bytes=MX_ALIGN),
                fmt,
            )

        def quantize_weights(n):
            nc.vector.quantize_mx(
                out=weight_codes[:, span(n, 1, WIDE)].bitcast(E4M3),
                scales=weight_scales[:, span(n, 1, WIDE)],
                in_=weights_bf[:, span(n, 1, WIDE * PACK)],
            )

        def quantize_moving(name):
            grouped, codes, scales, fmt = moving[name]
            nc.vector.quantize_mx(out=codes[:].bitcast(fmt), scales=scales[:], in_=grouped[:])

        interleave(on_scalar, moving["dy"][0][:], raw["dy"][:])
        deal(on_scalar, weights_bf[:, span(w_slot[0], 1, W * PACK)], raw["w"][:, :, span(0, 1, W)])
        deal(on_scalar, weights_bf[:, span(SLABS, 1, W * PACK)], raw["v"][:, :, span(0, 1, W)])
        interleave(on_scalar, moving["e"][0][:, E_ON_VECTOR * PACK :], raw["e"][:, :, E_ON_VECTOR:])
        quantize_moving("dy")
        deal(on_vector, weights_bf[:, span(w_slot[1], SLABS - 1, W * PACK)], raw["w"][:, :, span(1, SLABS - 1, W)])
        quantize_weights(0)
        deal(on_vector, weights_bf[:, span(SLABS + 1, SLABS - 1, W * PACK)], raw["v"][:, :, span(1, SLABS - 1, W)])
        quantize_weights(1)
        quantize_weights(2)
        interleave(on_vector, moving["e"][0][:, : E_ON_VECTOR * PACK], raw["e"][:, :, :E_ON_VECTOR])
        quantize_moving("e")

        banks = {}
        direct = BANKS - COPIED
        bank_order = [b for pair in zip(range(direct, BANKS), range(direct)) for b in pair]

        def mx_pass(a, b, first):
            if first:
                banks[b] = psum.tile([P, W], F32, name="bank%d" % b)
            j, h = divmod(b, HALVES)
            places = span((w_slot[a] if first else SLABS + a) * PACK + j, 1, P)
            codes, scales, fmt = moving["dy" if first else "e"][1:]
            nc.tensor.matmul_mx(
                out=banks[b][:],
                lhsT=weight_codes[:, places].bitcast(E4M3),
                lhsT_scale=weight_scales[:, places],
                rhs=codes[:, span(h, 1, W)].bitcast(fmt),
                rhs_scale=scales[:, span(h, 1, W)],
                start=first,
                stop=not first,
            )

        def multiply(in_place, sums):
            nc.vector.tensor_tensor(out=in_place, in0=sums, in1=in_place, op=mybir.AluOpType.mult)

        for b in bank_order:
            mx_pass(0, b, True)

        result_bf = keep.tile([P, SLABS * T * PACK], BF16, name="wide_bf", align_bytes=MX_ALIGN)
        copied = keep.tile([P, COPIED * W], F32)

        last = SLABS - 1
        for a in range(SLABS):
            flat = slabs[a][:].rearrange("p j t -> p (j t)")
            for b in bank_order:
                if a > 0:
                    mx_pass(a, b, True)
                mx_pass(a, b, False)
            if a == 0:
                for b in range(direct, BANKS):
                    on_scalar(out=copied[:, span(b - direct, 1, W)], in_=banks[b][:])
                for b in range(direct):
                    multiply(flat[:, span(b, 1, W)], banks[b][:])
                multiply(flat[:, span(direct, COPIED, W)], copied[:])
            else:
                for b in bank_order:
                    multiply(flat[:, span(b, 1, W)], banks[b][:])
            nc.sync.dma_start(out=by_partition(out_0[span(a, 1, W), :]), in_=slabs[a][:])
            if a < last:
                interleave(on_scalar, result_bf[:, span(a, 1, T * PACK)], slabs[a][:])

        def quantize_result(a):
            nc.vector.quantize_mx(
                out=out_codes[:, a, :].bitcast(E4M3), scales=out_scales[:, a, :], in_=result_bf[:, span(a, 1, T * PACK)]
            )

        def store_codes(first, count):
            nc.sync.dma_start(
                out=out_1[span(first, count, 1)].rearrange("a p t j -> p a (t j)").bitcast(I32),
                in_=out_codes[:, span(first, count, 1), :].bitcast(I32),
            )

        quantize_result(0)
        interleave(on_vector, result_bf[:, span(last, 1, T * PACK)], slabs[last][:])
        quantize_result(1)
        store_codes(0, last)
        quantize_result(last)
        store_codes(last, 1)

        scale_rows = out_2.bitcast(I32).rearrange("a (q r) t -> r q a t", r=PACK)
        for r in range(PACK):
            nc.sync.dma_start(out=scale_rows[r], in_=out_scales[r:P:QUADRANT, :, :].bitcast(I32))
